import numpy as np, ml_dtypes
CORES = [65,66,69,71,193,194,197,199,321,322,325,327,449,450,453,455]
N = 16
import mx_ref
NC, G, D = 128, 2, 8
C = np.float32(0.037)
BF = ml_dtypes.bfloat16
def cut(t, i, w=512):
    return t[:, w * i:w * i + w]
def tile(rs):
    return np.stack(rs, axis=2).reshape(128, -1).astype(BF)
def act(Z):
    return [np.maximum(s * z, 0) * C for z in Z for s in (1, -1)]
def taps(w, i, e):
    return mx_ref.matmul(mx_ref.quantize(cut(w, 2 * i)), mx_ref.quantize(e[:, :4 * NC])) + mx_ref.matmul(mx_ref.quantize(cut(w, 2 * i + 1)), mx_ref.quantize(e[:, 4 * D:4 * D + 4 * NC]))
def setup_inputs(rng):
    def f(*shape):
        return mx_ref.flush((rng.standard_normal(shape, dtype=np.float32) * np.exp2(rng.integers(-2, 3, shape[:-1] + (1,)))).astype(BF))
    return {"x": f(N, 128, 4 * NC), "wa": np.broadcast_to(f(1, 128, 2 * G * 512), (N, 128, 2 * G * 512)).copy(), "wb": f(N, 128, 2 * 512)}
def setup_inputs_blocks(rng):
    d = setup_inputs(rng)
    for k in ("x", "wb"): d[k] = mx_ref.spread(d[k], rng, 2)
    return d
def setup_inputs_wide(rng):
    d = setup_inputs(rng)
    for k in ("wb",): d[k] = mx_ref.flush((d[k].astype(np.float32) * np.exp2(rng.integers(-6, 7, (N, 1, 1))).astype(np.float32)).astype(BF))
    return d
def setup_inputs_zeros(rng):
    d = setup_inputs(rng); v = d["x"].reshape(N, 128, -1, 4).copy()
    v[np.broadcast_to((rng.random((N, 1, v.shape[2], 1)) < 0.33), v.shape)] = 0
    d["x"] = v.reshape(d["x"].shape)
    return d
def reference(x, wa, wb):
    edge = lambda t, r: np.concatenate([t[(r - 1) % N][:, 4 * (NC - D):], t[r]], axis=1)
    u = [tile(act([taps(wa[r], i, edge(x, r)) for i in range(G)])) for r in range(N)]
    y = np.zeros((N, 128, NC), np.float32)
    for r in range(N):
        y[r] = taps(wb[r], 0, edge(u, r))
    return {"y": y}

from concourse.mybir import dt, AluOpType, ActivationFunctionType

D, NC, H = 8, 128, 16
CF = 0.037
CODES = "float8_e4m3fn_x4"

SCRATCH = {
    "xt": ("sbuf", [128, 4 * NC], "bfloat16"),
    "wat": ("sbuf", [128, 4 * 512], "bfloat16"),
    "wbt": ("sbuf", [128, 2 * 512], "bfloat16"),
    "xh": ("sbuf", [128, H + NC], CODES),
    "xhs": ("sbuf", [128, H + NC], "uint8"),
    "xb": ("sbuf", [128, D + NC], CODES),
    "xbs": ("sbuf", [128, D + NC], "uint8"),
    "wq": ("sbuf", [128, 4 * 128], CODES),
    "wqs": ("sbuf", [128, 4 * 128], "uint8"),
    "vq": ("sbuf", [128, 2 * 128], CODES),
    "vqs": ("sbuf", [128, 2 * 128], "uint8"),
    "u": ("sbuf", [128, 4 * (D + NC)], "bfloat16"),
    "ub": ("sbuf", [128, D + NC], CODES),
    "ubs": ("sbuf", [128, D + NC], "uint8"),
    "uh": ("sbuf", [128, D + NC], CODES),
    "uhs": ("sbuf", [128, D + NC], "uint8"),
    "yb": ("sbuf", [128, NC - H], "float32"),
    "ye": ("sbuf", [128, H], "float32"),
    "pb0": ("psum", [128, 512], "float32"),
    "pb1": ("psum", [128, 512], "float32"),
    "pby": ("psum", [128, 512], "float32"),
    "pe0": ("psum", [128, 512], "float32"),
    "pe1": ("psum", [128, 512], "float32"),
    "pey": ("psum", [128, 512], "float32"),
}
SEMAPHORES = ["lx", "la0", "la1", "lb0", "lb1", "padu", "qxh", "qxp", "qxb", "qa0", "qa1", "qa2", "qa3", "qb0", "qb1",
              "arr", "sent", "zb0", "zb1", "rb0", "rb1", "qub", "zyb", "cyb", "dyb",
              "ze0", "ze1", "re0", "re1", "que", "zye", "cye", "dye"]


def engines(mask, n):
    out = 0
    for b in range(16):
        if mask >> b & 1 and n:
            out |= 1 << b
            n -= 1
    return out


def rank_program(g, core, T, topo):
    rank = T.rank_of(core)
    if rank is None:
        return
    s = T.sem
    dst = T.cores[(rank + 1) % len(T.cores)]
    mul, mx = AluOpType.mult, AluOpType.max
    relu = ActivationFunctionType.Relu

    for q, lo, a, b in ((g.sync, 0, 0, 0), (g.scalar, 64, 1, 1)):
        q.dma_start(T.xt[lo:lo + 64, :], T.x[lo:lo + 64, :]).then_inc(s.lx, 16)
        q.dma_start(T.wat[:, 1024 * a:1024 * a + 1024], T.wa[:, 1024 * a:1024 * a + 1024]).then_inc(s["la%d" % a], 16)
        q.dma_start(T.wbt[:, 512 * b:512 * b + 512], T.wb[:, 512 * b:512 * b + 512]).then_inc(s["lb%d" % b], 16)

    rid, pid = topo.addr(dst, core)
    m = engines(topo.mask(core, dst), 8)
    n = bin(m).count("1")
    g.wait_ge(s.qxh, 1)
    g.remote_dma(T.xh[:, 0:H].bitcast(dt.uint8), T.xh[:, NC:NC + H].bitcast(dt.uint8), s.arr, s.sent, pid, rid, m)
    g.remote_dma(T.xhs[:, 0:H], T.xhs[:, NC:NC + H], s.arr, s.sent, pid, rid, m)
    g.wait_ge(s.sent, 2 * n)

    v = g.vector
    v.memset(T.u[:, 0:8 * D], 0.0).then_inc(s.padu, 1)
    v.wait_ge(s.lx, 32)
    v.quantize_mx(T.xh[:, H:H + NC], T.xhs[:, H:H + NC], T.xt[:, :]).then_inc(s.qxh, 1)
    v.quantize_mx(T.xb[:, 0:NC], T.xbs[:, 0:NC], T.xt[:, :]).then_inc(s.qxp, 1)
    v.wait_ge(s.qxp, 1)
    v.quantize_mx(T.xb[:, D:D + NC], T.xbs[:, D:D + NC], T.xt[:, :]).then_inc(s.qxb, 1)
    for k in range(4):
        if k % 2 == 0:
            v.wait_ge(s["la%d" % (k // 2)], 16)
        c = slice(128 * k, 128 * k + 128)
        v.quantize_mx(T.wq[:, c], T.wqs[:, c], T.wat[:, 512 * k:512 * k + 512]).then_inc(s["qa%d" % k], 1)

    def v_acts(ps, sem_in, sem_out, lo, hi):
        v.wait_ge(sem_in, 1)
        for b, sg in ((2, CF), (3, -CF)):
            v.tensor_scalar(T.u[:, 4 * lo + b:4 * hi:4], ps, sg, 0.0, mul, mx).then_inc(sem_out, 1)

    def s_acts(ps, sem_in, sem_out, lo, hi):
        g.scalar.wait_ge(sem_in, 1)
        for b, sg in ((0, CF), (1, -CF)):
            g.scalar.activation(T.u[:, 4 * lo + b:4 * hi:4], ps, relu, scale=sg).then_inc(sem_out, 1)

    v_acts(T.pb1[:, D:NC], s.zb1, s.rb1, 2 * D, D + NC)
    for k in range(2):
        v.wait_ge(s["lb%d" % k], 16)
        c = slice(128 * k, 128 * k + 128)
        v.quantize_mx(T.vq[:, c], T.vqs[:, c], T.wbt[:, 512 * k:512 * k + 512]).then_inc(s["qb%d" % k], 1)
    v.wait_ge(s.padu, 1)
    v.wait_ge(s.rb0, 2)
    v.wait_ge(s.rb1, 2)
    v.quantize_mx(T.ub[:, :], T.ubs[:, :], T.u[:, :]).then_inc(s.qub, 1)
    v.wait_ge(s.qub, 1)
    v_acts(T.pe1[:, 0:2 * D], s.ze1, s.re1, 0, 2 * D)
    v.wait_ge(s.re0, 2)
    v.wait_ge(s.re1, 2)
    v.quantize_mx(T.uh[:, :], T.uhs[:, :], T.u[:, :]).then_inc(s.que, 1)
    v.wait_ge(s.zye, 1)
    v.tensor_copy(T.ye[:, :], T.pey[:, 0:H]).then_inc(s.cye, 1)

    s_acts(T.pb0[:, D:NC], s.zb0, s.rb0, 2 * D, D + NC)
    g.scalar.wait_ge(s.zyb, 1)
    g.scalar.activation(T.yb[:, :], T.pby[:, H:NC], ActivationFunctionType.Copy).then_inc(s.cyb, 1)
    g.scalar.wait_ge(s.qub, 1)
    s_acts(T.pe0[:, 0:2 * D], s.ze0, s.re0, 0, 2 * D)

    t = g.tensor

    def taps(out, w, ws, k, x, xs, sem):
        for tap in (0, 1):
            c = slice(128 * (k + tap), 128 * (k + tap) + 128)
            e = slice(D * tap, D * tap + NC)
            i = t.matmul_mx(out[:, 0:NC], w[:, c], ws[:, c], x[:, e], xs[:, e], tap == 0, tap == 1)
            if tap == 1:
                i.then_inc(sem, 1)

    t.wait_ge(s.qxb, 1)
    for i in range(2):
        t.wait_ge(s["qa%d" % (2 * i)], 1)
        t.wait_ge(s["qa%d" % (2 * i + 1)], 1)
        taps(T["pb%d" % i], T.wq, T.wqs, 2 * i, T.xb, T.xbs, s["zb%d" % i])
    t.wait_ge(s.qb0, 1)
    t.wait_ge(s.qb1, 1)
    t.wait_ge(s.qub, 1)
    taps(T.pby, T.vq, T.vqs, 0, T.ub, T.ubs, s.zyb)
    t.wait_ge(s.qxh, 1)
    t.wait_ge(s.arr, 2 * n_in(rank, T, topo))
    for i in range(2):
        taps(T["pe%d" % i], T.wq, T.wqs, 2 * i, T.xh, T.xhs, s["ze%d" % i])
    t.wait_ge(s.que, 1)
    taps(T.pey, T.vq, T.vqs, 0, T.uh, T.uhs, s.zye)

    g.sync.wait_ge(s.cyb, 1)
    g.sync.dma_start(T.y[:, H:NC], T.yb[:, :]).then_inc(s.dyb, 16)
    g.sync.wait_ge(s.cye, 1)
    g.sync.dma_start(T.y[:, 0:H], T.ye[:, :]).then_inc(s.dye, 16)
    g.sync.wait_ge(s.dyb, 16)
    g.sync.wait_ge(s.dye, 16)


def n_in(rank, T, topo):
    return bin(engines(topo.mask(T.cores[rank - 1], T.cores[rank]), 8)).count("1")
